import numpy as np
import ml_dtypes


def mxq(x, axis, fmt="e4m3"):
    dtype, down = {"e4m3": (ml_dtypes.float8_e4m3fn, 7), "e5m2": (ml_dtypes.float8_e5m2, 14)}[fmt]
    v = np.moveaxis(np.asarray(x, np.float32).astype(ml_dtypes.bfloat16).astype(np.float64), axis, -1)
    blocks = v.reshape(v.shape[:-1] + (-1, 32))
    amax = np.abs(blocks).max(-1, keepdims=True)
    byte = np.maximum(np.where(amax > 0, np.frexp(amax)[1] - 1 + 127, 0) - down, 1)
    scale = np.exp2(byte - 127.0)
    codes = (blocks / scale).astype(np.float32).astype(dtype).astype(np.float64)
    return np.moveaxis((codes * scale).reshape(v.shape), -1, axis)


WIDE = False


def mx_kscale(k):
    if not WIDE:
        return np.ones(k)
    levels = np.array([10, -10, 5, -5, 0])
    if k % 512:
        return np.exp2(np.random.permutation(np.resize(levels, k // 32))).repeat(32)
    a = np.empty((k // 512, 16))
    for p in range(k // 512):
        a[p, :8] = np.random.permutation(np.resize(levels, 8))
        for g in range(8):
            far = levels[np.abs(levels - a[p, g]) >= 10]
            a[p, g + 8] = far[np.random.randint(len(far))]
    return np.exp2(a.ravel()).repeat(32)


def f64(x):
    return np.asarray(x).astype(np.float64)


def striped(idx):
    return np.tile(idx.reshape(-1, 16).T, (8, 1)).astype(np.uint16)


def unstriped(offs):
    return offs[:16].T.reshape(-1).astype(np.int64)


def striped8(idx):
    return np.concatenate([x.reshape(-1, 16).T for x in idx]).astype(np.uint16)


def runs(offs, k):
    lists = np.stack([offs[16 * r : 16 * r + 16].T.reshape(-1) for r in range(8)]).astype(np.int64)
    return lists[np.arange(k) % 512 // 64]


def pack_weight(w):
    k, n = w.shape
    w = f64(np.asarray(w, np.float32).astype(ml_dtypes.bfloat16)).reshape(k // 32, 32, n)
    amax = np.abs(w).max(1)
    byte = np.clip(np.where(amax > 0, np.frexp(amax)[1] - 1 + 127 - 7, 1), 1, 254)
    scaled = (w * np.exp2(127.0 - byte)[:, None, :]).reshape(k, n).astype(np.float32)
    words = np.ascontiguousarray(scaled.reshape(k // 512, 128, 4, n).transpose(0, 1, 3, 2)).astype(ml_dtypes.float8_e4m3fn).view(np.uint8)
    return words, np.ascontiguousarray(byte.astype(np.uint8).reshape(k // 512, 16, n))


def unpack_weight(words, scales):
    g, p, n, _ = words.shape
    vals = np.ascontiguousarray(words).view(ml_dtypes.float8_e4m3fn).astype(np.float64) * np.repeat(np.exp2(scales.astype(np.float64) - 127.0), 8, axis=1)[..., None]
    return vals.transpose(0, 1, 3, 2).reshape(g * 512, n)


def relu(v):
    return np.maximum(v, 0.0)


K, T, S, N, G, H, U = 512, 2048, 512, 512, 2048, 512, 1024


def setup_inputs():
    n = np.random.standard_normal
    s = mx_kscale(K)[:, None]
    u = mx_kscale(S)
    packed_xT = pack_weight(n((K, T)) * s)
    packed_dT = pack_weight(n((K, G)) / s)
    perm = np.stack([np.random.permutation(U) for _ in range(8)])
    return {
        "x_words": packed_xT[0],
        "x_scales": packed_xT[1],
        "d_words": packed_dT[0],
        "d_scales": packed_dT[1],
        "gn": (np.random.uniform(0.5, 1.5, (H, 1)) * u[:, None]).astype(np.float32),
        "w1": (n((H, N)) / np.sqrt(H) / u[:, None]).astype(np.float32),
        "offs": striped(np.random.permutation(T)[:S]),
        "kidx": striped8(np.random.randint(0, G, (8, H))),
        "n1": striped8(np.stack([np.random.permutation(S) for _ in range(8)])),
        "n2": striped8(perm[:, :S]),
        "n3": striped8(perm[:, S:]),
        "n4": striped8(np.stack([np.random.permutation(S) for _ in range(8)])),
    }


def reference(x_words, x_scales, d_words, d_scales, gn, w1, offs, kidx, n1, n2, n3, n4):
    d_kidx = unpack_weight(d_words, d_scales)[np.arange(K)[:, None], runs(kidx, K)]
    xq = unpack_weight(x_words, x_scales)[:, unstriped(offs)]
    s = 0.0625 * (d_kidx.T @ xq)
    rl = relu(s)
    ds = np.zeros((H, S))
    ds[np.arange(H)[:, None], runs(n1, H)] = rl
    z = f64(gn) * (ds - (0.5 * s))
    h = mxq(f64(w1), 0, "e4m3").T @ mxq(z, 0, "e4m3")
    dn = np.minimum(h, h[np.arange(N)[:, None], runs(n4, N)])
    up = np.maximum(h, h[np.arange(N)[:, None], runs(n4, N)])
    ph = np.zeros((N, U))
    ph[np.arange(N)[:, None], runs(n2, N)] = up
    out = ph.copy()
    out[np.arange(N)[:, None], runs(n3, N)] = dn
    return out

@@ -1,0 +1,277 @@
+from contextlib import ExitStack
+
+import concourse.mybir as mybir
+from concourse.masks import make_identity
+
+K, T, S, N, G, H, U = 512, 2048, 512, 512, 2048, 512, 1024
+FLOPS = 2 * K * H * S + 2 * H * N * S
+
+F32 = mybir.dt.float32
+BF16 = mybir.dt.bfloat16
+I32 = mybir.dt.int32
+U32 = mybir.dt.uint32
+U16 = mybir.dt.uint16
+U8 = mybir.dt.uint8
+FP8X4 = mybir.dt.float8_e4m3fn_x4
+ACT = mybir.ActivationFunctionType
+ALU = mybir.AluOpType
+
+P = 128
+PACK = 4
+HALF = 256
+
+
+def tile_picked_keysendpagmx_none_p_kernel(
+    tc, x_words, x_scales, d_words, d_scales, gn, w1, offs, kidx, n1, n2, n3, n4, out
+):
+    nc = tc.nc
+    with ExitStack() as ctx:
+        keep = ctx.enter_context(tc.tile_pool(name="keep", bufs=1))
+        psum = ctx.enter_context(tc.psum_pool(name="psum", bufs=1))
+
+        def load_list(name, src):
+            tile = keep.tile([P, S // 16], U16, name=name)
+            nc.sync.dma_start(tile[:], src)
+            return tile
+
+        def cols(half):
+            return slice(half * HALF, (half + 1) * HALF)
+
+        def entries(tile, span):
+            return tile[:, span.start // 16 : span.stop // 16]
+
+        def bank(number, width):
+            return psum.tile([P, width], F32, name="bank%d" % number)
+
+        d_scale_table = keep.tile([P, G], U8, align_bytes=64)
+        x_scale_table = keep.tile([P, T], U8, align_bytes=64)
+        nc.vector.memset(d_scale_table[:].bitcast(I32), 0)
+        nc.vector.memset(x_scale_table[:].bitcast(I32), 0)
+        kidx_list = load_list("kidx_list", kidx)
+        offs_list = load_list("offs_list", offs)
+        nc.sync.dma_start(d_scale_table[0:P:8, :].bitcast(I32), d_scales[0].bitcast(I32))
+        nc.sync.dma_start(x_scale_table[0:P:8, :].bitcast(I32), x_scales[0].bitcast(I32))
+        n1_list = load_list("n1_list", n1)
+        n4_list = load_list("n4_list", n4)
+        n2_list = load_list("n2_list", n2)
+        d_word_table = keep.tile([P, G], U32, align_bytes=64)
+        nc.sync.dma_start(d_word_table[:].bitcast(I32), d_words[0].rearrange("p c r -> p (c r)").bitcast(I32))
+        x_word_table = keep.tile([P, T], U32, align_bytes=64)
+        nc.sync.dma_start(x_word_table[:].bitcast(I32), x_words[0].rearrange("p c r -> p (c r)").bitcast(I32))
+        n3_list = load_list("n3_list", n3)
+        gains = keep.tile([P, PACK], F32)
+        nc.sync.dma_start(gains[:], gn.rearrange("(p t) o -> p (t o)", t=PACK))
+
+        d_scale_picked = keep.tile([P, H], U8, align_bytes=64)
+        x_scale_picked = keep.tile([P, S], U8, align_bytes=64)
+        scale_plane = keep.tile([P, H + S], U8, align_bytes=64)
+        nc.vector.tensor_copy(d_scale_picked[:], d_scale_table[:].indirect(kidx_list[:]))
+        nc.vector.tensor_copy(x_scale_picked[:], x_scale_table[:].indirect(offs_list[:]))
+        nc.vector.tensor_copy(
+            scale_plane[:, :H].rearrange("p (t m) -> p m t", t=PACK),
+            d_scale_picked[:].rearrange("p (m t) -> p m t", t=PACK),
+        )
+        nc.vector.tensor_copy(scale_plane[:, H:], x_scale_picked[:])
+        for c in range(1, 4):
+            nc.scalar.dma_start(scale_plane[c:P:32, :].bitcast(I32), scale_plane[8 * c : P : 32, :].bitcast(I32))
+
+        x_word_picked = [keep.tile([P, HALF], U32, align_bytes=64, name="x_word_picked%d" % h) for h in range(2)]
+        d_word_picked = keep.tile([P, H], U32, align_bytes=64)
+        nc.vector.tensor_copy(d_word_picked[:], d_word_table[:].indirect(kidx_list[:]))
+        d_word_dealt = keep.tile([P, H], U32, align_bytes=64)
+        nc.vector.tensor_copy(
+            d_word_dealt[:].rearrange("p (t m) -> p m t", t=PACK),
+            d_word_picked[:].rearrange("p (m t) -> p m t", t=PACK),
+        )
+        for half in range(2):
+            nc.vector.tensor_copy(x_word_picked[half][:], x_word_table[:].indirect(entries(offs_list, cols(half))))
+
+        w_raw = keep.tile([P, PACK, N], F32, align_bytes=64, tag="d_word_table")
+        nc.sync.dma_start(w_raw[:], w1.rearrange("(p t) m -> p t m", t=PACK))
+
+        identity = keep.tile([P, P], F32)
+        make_identity(nc, identity[:])
+
+        def turn(dst, terms, span):
+            for start in range(span.start, span.stop, P):
+                block = slice(start, start + P)
+                for number, term in enumerate(terms):
+                    nc.tensor.matmul(
+                        dst[:, block],
+                        term[:, block],
+                        identity[:],
+                        start=(number == 0),
+                        stop=(number == len(terms) - 1),
+                        is_transpose=True,
+                    )
+
+        last = PACK - 1
+        whole = slice(0, S)
+        half_gain = keep.tile([P, 1], F32)
+        nc.gpsimd.tensor_scalar_mul(half_gain[:], gains[:, last : last + 1], 0.03125)
+
+        rl = [keep.tile([P, S], F32, name="rl%d" % t) for t in range(PACK)]
+        half_s = [keep.tile([P, S], F32, name="half_s%d" % t) for t in range(PACK)]
+        ds = [keep.tile([P, S if t < 2 else 2 * S], F32, name="ds%d" % t) for t in range(PACK)]
+        z_planes = keep.tile([P, PACK, S], BF16, align_bytes=64)
+
+        scores = {}
+
+        def score(t, half):
+            acc = bank(2 * t + half, HALF)
+            scores[t, half] = acc
+            nc.tensor.matmul_mx(
+                out=acc[:],
+                lhsT=d_word_dealt[:, t * P : (t + 1) * P].bitcast(FP8X4),
+                lhsT_scale=scale_plane[:, t * P : (t + 1) * P],
+                rhs=x_word_picked[half][:].bitcast(FP8X4),
+                rhs_scale=scale_plane[:, H + half * HALF : H + (half + 1) * HALF],
+                start=True,
+                stop=True,
+            )
+            nc.scalar.activation(rl[t][:, cols(half)], acc[:], ACT.Relu, scale=0.0625)
+
+        for half in range(2):
+            for t in range(2):
+                score(t, half)
+                nc.vector.tensor_copy(ds[t][:].indirect(entries(n1_list, cols(half))), rl[t][:, cols(half)])
+        for t in range(2, PACK):
+            for half in range(2):
+                score(t, half)
+            nc.vector.tensor_copy(ds[t][:].indirect(n1_list[:]), rl[t][:])
+
+        for t in range(PACK):
+            for half in range(2):
+                scale = half_gain[:] if t == last else -0.03125
+                nc.scalar.activation(half_s[t][:, cols(half)], scores[t, half][:], ACT.Copy, scale=scale)
+
+        w_grouped = keep.tile([P, N * PACK], BF16, align_bytes=64)
+        w_in = w_raw[:].rearrange("p t (m u) -> p m u t", u=PACK)
+        w_out = w_grouped[:].rearrange("p (u m t) -> p m u t", u=PACK, t=PACK)
+        for quarter in range(4):
+            rows = slice(32 * quarter, 32 * (quarter + 1))
+            nc.scalar.copy(w_out[:, rows], w_in[:, rows])
+        w_words_first = keep.tile([P, P], U32, align_bytes=64)
+        w_scale_first = keep.tile([P, P], U8, align_bytes=64)
+        nc.vector.quantize_mx(
+            out=w_words_first[:].bitcast(FP8X4), scales=w_scale_first[:], in_=w_grouped[:, : P * PACK]
+        )
+
+        for t in range(last):
+            difference = keep.tile([P, S], F32, name="difference%d" % t)
+            for half in (1, 0):
+                turned = bank(half, S)
+                turn(turned, (ds[t], half_s[t]), cols(half))
+                nc.scalar.copy(difference[:, cols(half)], turned[:, cols(half)])
+            for half in (1, 0):
+                back = bank(2 + half, S)
+                turn(back, (difference,), cols(half))
+                nc.scalar.activation(
+                    z_planes[:, t, cols(half)], back[:, cols(half)], ACT.Copy, scale=gains[:, t : t + 1]
+                )
+
+        z_words, z_scale, z_grouped = {}, {}, {}
+        for half in (1, 0):
+            nc.vector.scalar_tensor_tensor(
+                z_planes[:, last, cols(half)],
+                ds[last][:, cols(half)],
+                gains[:, last : last + 1],
+                half_s[last][:, cols(half)],
+                ALU.mult,
+                ALU.subtract,
+            )
+        for half in (1, 0):
+            z_grouped[half] = keep.tile([P, HALF * PACK], BF16, align_bytes=64, name="z_grouped%d" % half)
+            src = z_planes[:, :, cols(half)].rearrange("p t j -> p j t")
+            dst = z_grouped[half][:].rearrange("p (j t) -> p j t", t=PACK)
+            if half == 0:
+                nc.vector.tensor_copy(dst, src)
+            else:
+                nc.scalar.copy(dst, src)
+        for half in range(2):
+            z_words[half] = keep.tile([P, HALF], U32, align_bytes=64, name="z_words%d" % half)
+            z_scale[half] = keep.tile([P, HALF], U8, align_bytes=64, name="z_scale%d" % half)
+            nc.vector.quantize_mx(out=z_words[half][:].bitcast(FP8X4), scales=z_scale[half][:], in_=z_grouped[half][:])
+
+        w_words_rest = keep.tile([P, N - P], U32, align_bytes=64, tag="z_grouped1")
+        w_scale_rest = keep.tile([P, N - P], U8, align_bytes=64)
+        nc.vector.quantize_mx(out=w_words_rest[:].bitcast(FP8X4), scales=w_scale_rest[:], in_=w_grouped[:, P * PACK :])
+
+        def values_product(acc, t, half):
+            if t == 0:
+                words, scale = w_words_first[:], w_scale_first[:]
+            else:
+                words, scale = w_words_rest[:, (t - 1) * P : t * P], w_scale_rest[:, (t - 1) * P : t * P]
+            nc.tensor.matmul_mx(
+                out=acc,
+                lhsT=words.bitcast(FP8X4),
+                lhsT_scale=scale,
+                rhs=z_words[half][:].bitcast(FP8X4),
+                rhs_scale=z_scale[half][:],
+                start=True,
+                stop=True,
+            )
+
+        out_rows = out.rearrange("(p t) w -> t p w", t=PACK)
+        h = [keep.tile([P, S], F32, name="h%d" % t) for t in range(PACK)]
+        minus_h = {t: keep.tile([P, S], F32, name="minus_h%d" % t) for t in range(1, PACK)}
+        other = [keep.tile([P, S], F32, name="other%d" % t) for t in range(PACK)]
+        page = [keep.tile([P, U], F32, name="page%d" % t) for t in range(PACK)]
+
+        def fetch(t, half):
+            nc.scalar.activation(other[t][:, cols(half)], h[t][:].indirect(entries(n4_list, cols(half))), ACT.Copy)
+
+        def excess(t, span):
+            turned = bank(5, S)
+            turn(turned, (other[t], minus_h[t]), span)
+            positive = keep.tile([P, S], F32, name="positive%d" % t)
+            nc.scalar.activation(positive[:, span], turned[:, span], ACT.Relu)
+            back = bank((6 + t) % 8, S)
+            turn(back, (positive,), span)
+            return back
+
+        def send(t, span, back, sign, base, places):
+            delta = keep.tile([P, S], F32, tag="delta", bufs=2)
+            nc.scalar.activation(delta[:, span], back[:, span], ACT.Copy, scale=sign)
+            nc.vector.tensor_tensor(page[t][:].indirect(entries(places, span)), base[:, span], delta[:, span], ALU.add)
+
+        for half in range(2):
+            acc = bank(half, HALF)
+            values_product(acc[:], 0, half)
+            nc.scalar.copy(h[0][:, cols(half)], acc[:])
+        for half in range(2):
+            fetch(0, half)
+        up = keep.tile([P, S], F32)
+        dn = keep.tile([P, S], F32)
+
+        def extreme(dst, op, half):
+            nc.vector.tensor_tensor(dst[:, cols(half)], h[0][:, cols(half)], other[0][:, cols(half)], op)
+
+        def place(src, places, half):
+            nc.vector.tensor_copy(page[0][:].indirect(entries(places, cols(half))), src[:, cols(half)])
+
+        extreme(up, ALU.max, 0)
+        extreme(dn, ALU.min, 0)
+        place(up, n2_list, 0)
+        extreme(up, ALU.max, 1)
+        place(dn, n3_list, 0)
+        extreme(dn, ALU.min, 1)
+        place(up, n2_list, 1)
+        place(dn, n3_list, 1)
+        nc.sync.dma_start(out_rows[0], page[0][:])
+
+        backs = {}
+        for t in range(1, PACK + 1):
+            if t < PACK:
+                acc = bank(1 + t, S)
+                for half in range(2):
+                    values_product(acc[:, cols(half)], t, half)
+                nc.scalar.copy(h[t][:], acc[:])
+                for half in range(2):
+                    fetch(t, half)
+                nc.scalar.activation(minus_h[t][:], acc[:], ACT.Copy, scale=-1.0)
+                backs[t] = excess(t, whole)
+                send(t, whole, backs[t], 1.0, h[t], n2_list)
+            if t > 1:
+                send(t - 1, whole, backs[t - 1], -1.0, other[t - 1], n3_list)
+                nc.sync.dma_start(out_rows[t - 1], page[t - 1][:])

@@ -19,6 +19,7 @@ ALU = mybir.AluOpType
 P = 128
 PACK = 4
 HALF = 256
+D_SPLIT = 1024
 
 
 def tile_picked_keysendpagmx_none_p_kernel(
@@ -55,7 +56,9 @@ def tile_picked_keysendpagmx_none_p_kernel(
         n4_list = load_list("n4_list", n4)
         n2_list = load_list("n2_list", n2)
         d_word_table = keep.tile([P, G], U32, align_bytes=64)
-        nc.sync.dma_start(d_word_table[:].bitcast(I32), d_words[0].rearrange("p c r -> p (c r)").bitcast(I32))
+        d_word_rows = d_words[0].rearrange("p c r -> p (c r)").bitcast(I32)
+        nc.sync.dma_start(d_word_table[:, :D_SPLIT].bitcast(I32), d_word_rows[:, :D_SPLIT])
+        nc.sync.dma_start(d_word_table[:, D_SPLIT:].bitcast(I32), d_word_rows[:, D_SPLIT:])
         x_word_table = keep.tile([P, T], U32, align_bytes=64)
         nc.sync.dma_start(x_word_table[:].bitcast(I32), x_words[0].rearrange("p c r -> p (c r)").bitcast(I32))
         n3_list = load_list("n3_list", n3)
@@ -64,16 +67,16 @@ def tile_picked_keysendpagmx_none_p_kernel(
 
         d_scale_picked = keep.tile([P, H], U8, align_bytes=64)
         x_scale_picked = keep.tile([P, S], U8, align_bytes=64)
-        scale_plane = keep.tile([P, H + S], U8, align_bytes=64)
         nc.vector.tensor_copy(d_scale_picked[:], d_scale_table[:].indirect(kidx_list[:]))
         nc.vector.tensor_copy(x_scale_picked[:], x_scale_table[:].indirect(offs_list[:]))
+        scale_plane = keep.tile([P, H + S], U8, align_bytes=64, tag="x_scale_table")
         nc.vector.tensor_copy(
-            scale_plane[:, :H].rearrange("p (t m) -> p m t", t=PACK),
-            d_scale_picked[:].rearrange("p (m t) -> p m t", t=PACK),
+            scale_plane[:, :H].rearrange("p (t m) -> p t m", t=PACK),
+            d_scale_picked[:].rearrange("p (m t) -> p t m", t=PACK),
         )
-        nc.vector.tensor_copy(scale_plane[:, H:], x_scale_picked[:])
+        nc.vector.tensor_copy(scale_plane[:, H:].bitcast(I32), x_scale_picked[:].bitcast(I32))
         for c in range(1, 4):
-            nc.scalar.dma_start(scale_plane[c:P:32, :].bitcast(I32), scale_plane[8 * c : P : 32, :].bitcast(I32))
+            nc.sync.dma_start(scale_plane[c:P:32, :].bitcast(I32), scale_plane[8 * c : P : 32, :].bitcast(I32))
 
         x_word_picked = [keep.tile([P, HALF], U32, align_bytes=64, name="x_word_picked%d" % h) for h in range(2)]
         d_word_picked = keep.tile([P, H], U32, align_bytes=64)
@@ -107,8 +110,6 @@ def tile_picked_keysendpagmx_none_p_kernel(
 
         last = PACK - 1
         whole = slice(0, S)
-        half_gain = keep.tile([P, 1], F32)
-        nc.gpsimd.tensor_scalar_mul(half_gain[:], gains[:, last : last + 1], 0.03125)
 
         rl = [keep.tile([P, S], F32, name="rl%d" % t) for t in range(PACK)]
         half_s = [keep.tile([P, S], F32, name="half_s%d" % t) for t in range(PACK)]
@@ -142,22 +143,22 @@ def tile_picked_keysendpagmx_none_p_kernel(
 
         for t in range(PACK):
             for half in range(2):
-                scale = half_gain[:] if t == last else -0.03125
-                nc.scalar.activation(half_s[t][:, cols(half)], scores[t, half][:], ACT.Copy, scale=scale)
+                nc.scalar.activation(half_s[t][:, cols(half)], scores[t, half][:], ACT.Copy, scale=-0.03125)
+        gained_half_s = keep.tile([P, S], F32)
+        nc.scalar.activation(gained_half_s[:], half_s[last][:], ACT.Copy, scale=gains[:, last : last + 1])
 
         w_grouped = keep.tile([P, N * PACK], BF16, align_bytes=64)
         w_in = w_raw[:].rearrange("p t (m u) -> p m u t", u=PACK)
         w_out = w_grouped[:].rearrange("p (u m t) -> p m u t", u=PACK, t=PACK)
-        for quarter in range(4):
-            rows = slice(32 * quarter, 32 * (quarter + 1))
-            nc.scalar.copy(w_out[:, rows], w_in[:, rows])
-        w_words_first = keep.tile([P, P], U32, align_bytes=64)
-        w_scale_first = keep.tile([P, P], U8, align_bytes=64)
-        nc.vector.quantize_mx(
-            out=w_words_first[:].bitcast(FP8X4), scales=w_scale_first[:], in_=w_grouped[:, : P * PACK]
-        )
+
+        def round_weights(quarters):
+            for quarter in quarters:
+                rows = slice(32 * quarter, 32 * (quarter + 1))
+                nc.scalar.copy(w_out[:, rows], w_in[:, rows])
 
         for t in range(last):
+            if t != 1:
+                round_weights((t, t + 1))
             difference = keep.tile([P, S], F32, name="difference%d" % t)
             for half in (1, 0):
                 turned = bank(half, S)
@@ -170,20 +171,26 @@ def tile_picked_keysendpagmx_none_p_kernel(
                     z_planes[:, t, cols(half)], back[:, cols(half)], ACT.Copy, scale=gains[:, t : t + 1]
                 )
 
+        w_words_first = keep.tile([P, P], U32, align_bytes=64)
+        w_scale_first = keep.tile([P, P], U8, align_bytes=64)
+        nc.vector.quantize_mx(
+            out=w_words_first[:].bitcast(FP8X4), scales=w_scale_first[:], in_=w_grouped[:, : P * PACK]
+        )
+
         z_words, z_scale, z_grouped = {}, {}, {}
         for half in (1, 0):
             nc.vector.scalar_tensor_tensor(
                 z_planes[:, last, cols(half)],
                 ds[last][:, cols(half)],
                 gains[:, last : last + 1],
-                half_s[last][:, cols(half)],
+                gained_half_s[:, cols(half)],
                 ALU.mult,
-                ALU.subtract,
+                ALU.add,
             )
         for half in (1, 0):
             z_grouped[half] = keep.tile([P, HALF * PACK], BF16, align_bytes=64, name="z_grouped%d" % half)
-            src = z_planes[:, :, cols(half)].rearrange("p t j -> p j t")
-            dst = z_grouped[half][:].rearrange("p (j t) -> p j t", t=PACK)
+            src = z_planes[:, :, cols(half)].rearrange("p t (c i) -> p c t i", i=4)
+            dst = z_grouped[half][:].rearrange("p (c i t) -> p c t i", i=4, t=PACK)
             if half == 0:
                 nc.vector.tensor_copy(dst, src)
             else:

from contextlib import ExitStack

import concourse.mybir as mybir
from concourse.masks import make_identity

K, T, S, N, G, H, U = 512, 2048, 512, 512, 2048, 512, 1024
FLOPS = 2 * K * H * S + 2 * H * N * S

F32 = mybir.dt.float32
BF16 = mybir.dt.bfloat16
I32 = mybir.dt.int32
U32 = mybir.dt.uint32
U16 = mybir.dt.uint16
U8 = mybir.dt.uint8
FP8X4 = mybir.dt.float8_e4m3fn_x4
ACT = mybir.ActivationFunctionType
ALU = mybir.AluOpType

P = 128
PACK = 4
HALF = 256
D_SPLIT = 1024


def tile_picked_keysendpagmx_none_p_kernel(
    tc, x_words, x_scales, d_words, d_scales, gn, w1, offs, kidx, n1, n2, n3, n4, out
):
    nc = tc.nc
    with ExitStack() as ctx:
        keep = ctx.enter_context(tc.tile_pool(name="keep", bufs=1))
        psum = ctx.enter_context(tc.psum_pool(name="psum", bufs=1))

        def load_list(name, src):
            tile = keep.tile([P, S // 16], U16, name=name)
            nc.sync.dma_start(tile[:], src)
            return tile

        def cols(half):
            return slice(half * HALF, (half + 1) * HALF)

        def entries(tile, span):
            return tile[:, span.start // 16 : span.stop // 16]

        def bank(number, width):
            return psum.tile([P, width], F32, name="bank%d" % number)

        d_scale_table = keep.tile([P, G], U8, align_bytes=64)
        x_scale_table = keep.tile([P, T], U8, align_bytes=64)
        nc.vector.memset(d_scale_table[:].bitcast(I32), 0)
        nc.vector.memset(x_scale_table[:].bitcast(I32), 0)
        kidx_list = load_list("kidx_list", kidx)
        offs_list = load_list("offs_list", offs)
        nc.sync.dma_start(d_scale_table[0:P:8, :].bitcast(I32), d_scales[0].bitcast(I32))
        nc.sync.dma_start(x_scale_table[0:P:8, :].bitcast(I32), x_scales[0].bitcast(I32))
        n1_list = load_list("n1_list", n1)
        n4_list = load_list("n4_list", n4)
        n2_list = load_list("n2_list", n2)
        d_word_table = keep.tile([P, G], U32, align_bytes=64)
        d_word_rows = d_words[0].rearrange("p c r -> p (c r)").bitcast(I32)
        nc.sync.dma_start(d_word_table[:, :D_SPLIT].bitcast(I32), d_word_rows[:, :D_SPLIT])
        nc.sync.dma_start(d_word_table[:, D_SPLIT:].bitcast(I32), d_word_rows[:, D_SPLIT:])
        x_word_table = keep.tile([P, T], U32, align_bytes=64)
        nc.sync.dma_start(x_word_table[:].bitcast(I32), x_words[0].rearrange("p c r -> p (c r)").bitcast(I32))
        n3_list = load_list("n3_list", n3)
        gains = keep.tile([P, PACK], F32)
        nc.sync.dma_start(gains[:], gn.rearrange("(p t) o -> p (t o)", t=PACK))

        d_scale_picked = keep.tile([P, H], U8, align_bytes=64)
        x_scale_picked = keep.tile([P, S], U8, align_bytes=64)
        nc.vector.tensor_copy(d_scale_picked[:], d_scale_table[:].indirect(kidx_list[:]))
        nc.vector.tensor_copy(x_scale_picked[:], x_scale_table[:].indirect(offs_list[:]))
        scale_plane = keep.tile([P, H + S], U8, align_bytes=64, tag="x_scale_table")
        nc.vector.tensor_copy(
            scale_plane[:, :H].rearrange("p (t m) -> p t m", t=PACK),
            d_scale_picked[:].rearrange("p (m t) -> p t m", t=PACK),
        )
        nc.vector.tensor_copy(scale_plane[:, H:].bitcast(I32), x_scale_picked[:].bitcast(I32))
        for c in range(1, 4):
            nc.sync.dma_start(scale_plane[c:P:32, :].bitcast(I32), scale_plane[8 * c : P : 32, :].bitcast(I32))

        x_word_picked = [keep.tile([P, HALF], U32, align_bytes=64, name="x_word_picked%d" % h) for h in range(2)]
        d_word_picked = keep.tile([P, H], U32, align_bytes=64)
        nc.vector.tensor_copy(d_word_picked[:], d_word_table[:].indirect(kidx_list[:]))
        d_word_dealt = keep.tile([P, H], U32, align_bytes=64)
        nc.vector.tensor_copy(
            d_word_dealt[:].rearrange("p (t m) -> p m t", t=PACK),
            d_word_picked[:].rearrange("p (m t) -> p m t", t=PACK),
        )
        for half in range(2):
            nc.vector.tensor_copy(x_word_picked[half][:], x_word_table[:].indirect(entries(offs_list, cols(half))))

        w_raw = keep.tile([P, PACK, N], F32, align_bytes=64, tag="d_word_table")
        nc.sync.dma_start(w_raw[:], w1.rearrange("(p t) m -> p t m", t=PACK))

        identity = keep.tile([P, P], F32)
        make_identity(nc, identity[:])

        def turn(dst, terms, span):
            for start in range(span.start, span.stop, P):
                block = slice(start, start + P)
                for number, term in enumerate(terms):
                    nc.tensor.matmul(
                        dst[:, block],
                        term[:, block],
                        identity[:],
                        start=(number == 0),
                        stop=(number == len(terms) - 1),
                        is_transpose=True,
                    )

        last = PACK - 1
        whole = slice(0, S)

        rl = [keep.tile([P, S], F32, name="rl%d" % t) for t in range(PACK)]
        half_s = [keep.tile([P, S], F32, name="half_s%d" % t) for t in range(PACK)]
        ds = [keep.tile([P, S if t < 2 else 2 * S], F32, name="ds%d" % t) for t in range(PACK)]
        z_planes = keep.tile([P, PACK, S], BF16, align_bytes=64)

        scores = {}

        def score(t, half):
            acc = bank(2 * t + half, HALF)
            scores[t, half] = acc
            nc.tensor.matmul_mx(
                out=acc[:],
                lhsT=d_word_dealt[:, t * P : (t + 1) * P].bitcast(FP8X4),
                lhsT_scale=scale_plane[:, t * P : (t + 1) * P],
                rhs=x_word_picked[half][:].bitcast(FP8X4),
                rhs_scale=scale_plane[:, H + half * HALF : H + (half + 1) * HALF],
                start=True,
                stop=True,
            )
            nc.scalar.activation(rl[t][:, cols(half)], acc[:], ACT.Relu, scale=0.0625)

        for half in range(2):
            for t in range(2):
                score(t, half)
                nc.vector.tensor_copy(ds[t][:].indirect(entries(n1_list, cols(half))), rl[t][:, cols(half)])
        for t in range(2, PACK):
            for half in range(2):
                score(t, half)
            nc.vector.tensor_copy(ds[t][:].indirect(n1_list[:]), rl[t][:])

        for t in range(PACK):
            for half in range(2):
                nc.scalar.activation(half_s[t][:, cols(half)], scores[t, half][:], ACT.Copy, scale=-0.03125)
        gained_half_s = keep.tile([P, S], F32)
        nc.scalar.activation(gained_half_s[:], half_s[last][:], ACT.Copy, scale=gains[:, last : last + 1])

        w_grouped = keep.tile([P, N * PACK], BF16, align_bytes=64)
        w_in = w_raw[:].rearrange("p t (m u) -> p m u t", u=PACK)
        w_out = w_grouped[:].rearrange("p (u m t) -> p m u t", u=PACK, t=PACK)

        def round_weights(quarters):
            for quarter in quarters:
                rows = slice(32 * quarter, 32 * (quarter + 1))
                nc.scalar.copy(w_out[:, rows], w_in[:, rows])

        for t in range(last):
            if t != 1:
                round_weights((t, t + 1))
            difference = keep.tile([P, S], F32, name="difference%d" % t)
            for half in (1, 0):
                turned = bank(half, S)
                turn(turned, (ds[t], half_s[t]), cols(half))
                nc.scalar.copy(difference[:, cols(half)], turned[:, cols(half)])
            for half in (1, 0):
                back = bank(2 + half, S)
                turn(back, (difference,), cols(half))
                nc.scalar.activation(
                    z_planes[:, t, cols(half)], back[:, cols(half)], ACT.Copy, scale=gains[:, t : t + 1]
                )

        w_words_first = keep.tile([P, P], U32, align_bytes=64)
        w_scale_first = keep.tile([P, P], U8, align_bytes=64)
        nc.vector.quantize_mx(
            out=w_words_first[:].bitcast(FP8X4), scales=w_scale_first[:], in_=w_grouped[:, : P * PACK]
        )

        z_words, z_scale, z_grouped = {}, {}, {}
        for half in (1, 0):
            nc.vector.scalar_tensor_tensor(
                z_planes[:, last, cols(half)],
                ds[last][:, cols(half)],
                gains[:, last : last + 1],
                gained_half_s[:, cols(half)],
                ALU.mult,
                ALU.add,
            )
        for half in (1, 0):
            z_grouped[half] = keep.tile([P, HALF * PACK], BF16, align_bytes=64, name="z_grouped%d" % half)
            src = z_planes[:, :, cols(half)].rearrange("p t (c i) -> p c t i", i=4)
            dst = z_grouped[half][:].rearrange("p (c i t) -> p c t i", i=4, t=PACK)
            if half == 0:
                nc.vector.tensor_copy(dst, src)
            else:
                nc.scalar.copy(dst, src)
        for half in range(2):
            z_words[half] = keep.tile([P, HALF], U32, align_bytes=64, name="z_words%d" % half)
            z_scale[half] = keep.tile([P, HALF], U8, align_bytes=64, name="z_scale%d" % half)
            nc.vector.quantize_mx(out=z_words[half][:].bitcast(FP8X4), scales=z_scale[half][:], in_=z_grouped[half][:])

        w_words_rest = keep.tile([P, N - P], U32, align_bytes=64, tag="z_grouped1")
        w_scale_rest = keep.tile([P, N - P], U8, align_bytes=64)
        nc.vector.quantize_mx(out=w_words_rest[:].bitcast(FP8X4), scales=w_scale_rest[:], in_=w_grouped[:, P * PACK :])

        def values_product(acc, t, half):
            if t == 0:
                words, scale = w_words_first[:], w_scale_first[:]
            else:
                words, scale = w_words_rest[:, (t - 1) * P : t * P], w_scale_rest[:, (t - 1) * P : t * P]
            nc.tensor.matmul_mx(
                out=acc,
                lhsT=words.bitcast(FP8X4),
                lhsT_scale=scale,
                rhs=z_words[half][:].bitcast(FP8X4),
                rhs_scale=z_scale[half][:],
                start=True,
                stop=True,
            )

        out_rows = out.rearrange("(p t) w -> t p w", t=PACK)
        h = [keep.tile([P, S], F32, name="h%d" % t) for t in range(PACK)]
        minus_h = {t: keep.tile([P, S], F32, name="minus_h%d" % t) for t in range(1, PACK)}
        other = [keep.tile([P, S], F32, name="other%d" % t) for t in range(PACK)]
        page = [keep.tile([P, U], F32, name="page%d" % t) for t in range(PACK)]

        def fetch(t, half):
            nc.scalar.activation(other[t][:, cols(half)], h[t][:].indirect(entries(n4_list, cols(half))), ACT.Copy)

        def excess(t, span):
            turned = bank(5, S)
            turn(turned, (other[t], minus_h[t]), span)
            positive = keep.tile([P, S], F32, name="positive%d" % t)
            nc.scalar.activation(positive[:, span], turned[:, span], ACT.Relu)
            back = bank((6 + t) % 8, S)
            turn(back, (positive,), span)
            return back

        def send(t, span, back, sign, base, places):
            delta = keep.tile([P, S], F32, tag="delta", bufs=2)
            nc.scalar.activation(delta[:, span], back[:, span], ACT.Copy, scale=sign)
            nc.vector.tensor_tensor(page[t][:].indirect(entries(places, span)), base[:, span], delta[:, span], ALU.add)

        for half in range(2):
            acc = bank(half, HALF)
            values_product(acc[:], 0, half)
            nc.scalar.copy(h[0][:, cols(half)], acc[:])
        for half in range(2):
            fetch(0, half)
        up = keep.tile([P, S], F32)
        dn = keep.tile([P, S], F32)

        def extreme(dst, op, half):
            nc.vector.tensor_tensor(dst[:, cols(half)], h[0][:, cols(half)], other[0][:, cols(half)], op)

        def place(src, places, half):
            nc.vector.tensor_copy(page[0][:].indirect(entries(places, cols(half))), src[:, cols(half)])

        extreme(up, ALU.max, 0)
        extreme(dn, ALU.min, 0)
        place(up, n2_list, 0)
        extreme(up, ALU.max, 1)
        place(dn, n3_list, 0)
        extreme(dn, ALU.min, 1)
        place(up, n2_list, 1)
        place(dn, n3_list, 1)
        nc.sync.dma_start(out_rows[0], page[0][:])

        backs = {}
        for t in range(1, PACK + 1):
            if t < PACK:
                acc = bank(1 + t, S)
                for half in range(2):
                    values_product(acc[:, cols(half)], t, half)
                nc.scalar.copy(h[t][:], acc[:])
                for half in range(2):
                    fetch(t, half)
                nc.scalar.activation(minus_h[t][:], acc[:], ACT.Copy, scale=-1.0)
                backs[t] = excess(t, whole)
                send(t, whole, backs[t], 1.0, h[t], n2_list)
            if t > 1:
                send(t - 1, whole, backs[t - 1], -1.0, other[t - 1], n3_list)
                nc.sync.dma_start(out_rows[t - 1], page[t - 1][:])
